import numpy as np
import ml_dtypes


def mxq(x, axis, fmt="e4m3"):
    dtype, down = {"e4m3": (ml_dtypes.float8_e4m3fn, 7), "e5m2": (ml_dtypes.float8_e5m2, 14)}[fmt]
    v = np.moveaxis(np.asarray(x, np.float32).astype(ml_dtypes.bfloat16).astype(np.float64), axis, -1)
    blocks = v.reshape(v.shape[:-1] + (-1, 32))
    amax = np.abs(blocks).max(-1, keepdims=True)
    byte = np.maximum(np.where(amax > 0, np.frexp(amax)[1] - 1 + 127, 0) - down, 1)
    scale = np.exp2(byte - 127.0)
    codes = (blocks / scale).astype(np.float32).astype(dtype).astype(np.float64)
    return np.moveaxis((codes * scale).reshape(v.shape), -1, axis)


WIDE = False


def mx_kscale(k):
    if not WIDE:
        return np.ones(k)
    levels = np.array([10, -10, 5, -5, 0])
    if k % 512:
        return np.exp2(np.random.permutation(np.resize(levels, k // 32))).repeat(32)
    a = np.empty((k // 512, 16))
    for p in range(k // 512):
        a[p, :8] = np.random.permutation(np.resize(levels, 8))
        for g in range(8):
            far = levels[np.abs(levels - a[p, g]) >= 10]
            a[p, g + 8] = far[np.random.randint(len(far))]
    return np.exp2(a.ravel()).repeat(32)


def f64(x):
    return np.asarray(x).astype(np.float64)


def striped8(idx):
    return np.concatenate([x.reshape(-1, 16).T for x in idx]).astype(np.uint16)


def runs(offs, k):
    lists = np.stack([offs[16 * r : 16 * r + 16].T.reshape(-1) for r in range(8)]).astype(np.int64)
    return lists[np.arange(k) % 512 // 64]


def pack_weight(w):
    k, n = w.shape
    w = f64(np.asarray(w, np.float32).astype(ml_dtypes.bfloat16)).reshape(k // 32, 32, n)
    amax = np.abs(w).max(1)
    byte = np.clip(np.where(amax > 0, np.frexp(amax)[1] - 1 + 127 - 7, 1), 1, 254)
    scaled = (w * np.exp2(127.0 - byte)[:, None, :]).reshape(k, n).astype(np.float32)
    words = np.ascontiguousarray(scaled.reshape(k // 512, 128, 4, n).transpose(0, 1, 3, 2)).astype(ml_dtypes.float8_e4m3fn).view(np.uint8)
    return words, np.ascontiguousarray(byte.astype(np.uint8).reshape(k // 512, 16, n))


def unpack_weight(words, scales):
    g, p, n, _ = words.shape
    vals = np.ascontiguousarray(words).view(ml_dtypes.float8_e4m3fn).astype(np.float64) * np.repeat(np.exp2(scales.astype(np.float64) - 127.0), 8, axis=1)[..., None]
    return vals.transpose(0, 1, 3, 2).reshape(g * 512, n)


def sigmoid(v):
    return 1.0 / (1.0 + np.exp(-np.maximum(v, -700.0)))


K, T, S, H, U, C = 512, 2048, 512, 512, 1024, 512


def setup_inputs():
    n = np.random.standard_normal
    s = mx_kscale(K)[:, None]
    packed_xT = pack_weight(n((K, T)) * s)
    return {
        "x_words": packed_xT[0],
        "x_scales": packed_xT[1],
        "w1": (n((K, H)) / np.sqrt(K) / s).astype(np.float32),
        "mem": n((H, U)).astype(np.float32),
        "gs": (np.random.uniform(0.5, 1.5, (K, 1)) / s).astype(np.float32),
        "offs": striped8(np.random.randint(0, T, (8, S))),
        "n1": striped8(np.stack([np.random.permutation(U)[:S] for _ in range(8)])),
        "cand": striped8(np.random.randint(0, T, (8, C))),
        "n2": striped8(np.stack([np.random.permutation(U) for _ in range(8)])),
        "n3": striped8(np.stack([np.random.permutation(U) for _ in range(8)])),
    }


def reference(x_words, x_scales, w1, mem, gs, offs, n1, cand, n2, n3):
    x_cand = unpack_weight(x_words, x_scales)[np.arange(K)[:, None], runs(cand, K)]
    old = f64(mem)[np.arange(H)[:, None], runs(n1, H)]
    xq = unpack_weight(x_words, x_scales)[np.arange(K)[:, None], runs(offs, K)]
    y = mxq(f64(w1), 0, "e4m3").T @ xq
    nw = old + sigmoid(y) * (y - old)
    pg = f64(mem).copy()
    pg[np.arange(H)[:, None], runs(n1, H)] = nw
    z = f64(gs) * pg
    s = 0.0625 * ((x_cand.T @ mxq(z, 0, "e4m3")))
    return np.maximum(s * (sigmoid(s[np.arange(C)[:, None], runs(n2, C)])), s[np.arange(C)[:, None], runs(n3, C)])

@@ -1,0 +1,218 @@
+from contextlib import ExitStack
+
+import concourse.mybir as mybir
+
+F32 = mybir.dt.float32
+BF16 = mybir.dt.bfloat16
+I32 = mybir.dt.int32
+U32 = mybir.dt.uint32
+U16 = mybir.dt.uint16
+U8 = mybir.dt.uint8
+FP8X4 = mybir.dt.float8_e4m3fn_x4
+ACT = mybir.ActivationFunctionType
+ALU = mybir.AluOpType
+
+P = 128
+PACK = 4
+K, T, S, H, U, C = 512, 2048, 512, 512, 1024, 512
+HALF = U // 2
+FLOPS = 2 * K * H * S + 2 * K * C * U
+ORDER = (2, 0, 1, 3)
+
+
+def tile_picked_hcandpagetgmax_none_p_kernel(tc, x_words, x_scales, w1, mem, gs, offs, n1, cand, n2, n3, out):
+    nc = tc.nc
+    first, last = ORDER[0], ORDER[-1]
+    with ExitStack() as ctx:
+        keep = ctx.enter_context(tc.tile_pool(name="keep", bufs=1))
+        work = ctx.enter_context(tc.tile_pool(name="work", bufs=1))
+        psum = ctx.enter_context(tc.psum_pool(name="psum", bufs=1))
+
+        def load_list(name, src):
+            tile = keep.tile(list(src.shape), U16, name=name)
+            nc.sync.dma_start(tile[:], src)
+            return tile
+
+        scale_table = keep.tile([P, T], U8, name="scale_table", align_bytes=64)
+        nc.vector.memset(scale_table[:].bitcast(I32), 0)
+        scale_rows = x_scales[0].rearrange("(r e) c -> r e c", e=2)
+        for e in range(2):
+            nc.scalar.dma_start(scale_table[e:P:16, :].bitcast(I32), scale_rows[:, e, :].bitcast(I32))
+
+        offs_list = load_list("offs_list", offs)
+        w_rows = w1.rearrange("(p j) c -> p j c", j=PACK)
+        w_raw = []
+        for h in range(2):
+            tile = work.tile([P, PACK, H // 2], F32, name="w_raw%d" % h, tag="slot%d" % h, align_bytes=64)
+            nc.sync.dma_start(tile[:], w_rows[:, :, h * (H // 2) : (h + 1) * (H // 2)])
+            w_raw.append(tile)
+        cand_list = load_list("cand_list", cand)
+        n1_list = load_list("n1_list", n1)
+        gains = keep.tile([P, PACK], F32, name="gains")
+        nc.sync.dma_start(gains[:], gs.rearrange("(p t) o -> p (t o)", t=PACK))
+        word_table = keep.tile([P, T], U32, name="word_table", align_bytes=64)
+        nc.sync.dma_start(word_table[:].bitcast(I32), x_words[0].rearrange("p n t -> p (n t)").bitcast(I32))
+        n2_list = load_list("n2_list", n2)
+        n3_list = load_list("n3_list", n3)
+
+        warm_in = keep.tile([P, 1], F32, name="warm_in")
+        nc.vector.memset(warm_in[:], 0.0)
+        warm = keep.tile([P, 2], F32, name="warm")
+        nc.scalar.activation(warm[:, 0:1], warm_in[:], ACT.Silu)
+
+        def place_scale_rows(name, picked, queue):
+            plane = keep.tile([P, S], U8, name=name, align_bytes=64)
+            nc.vector.tensor_copy(plane[:].bitcast(I32), picked[:].bitcast(I32))
+            for e in range(2):
+                queue.dma_start(plane[2 + e : P : 32, :].bitcast(I32), picked[16 + e : P : 32, :].bitcast(I32))
+            return plane
+
+        offs_bytes = work.tile([P, S], U8, name="offs_bytes", tag="slot2", align_bytes=64)
+        nc.vector.tensor_copy(offs_bytes[:], scale_table[:].indirect(offs_list[:]))
+        offs_scales = place_scale_rows("offs_scales", offs_bytes, nc.scalar)
+
+        w_grouped = work.tile([P, PACK, P, PACK], BF16, name="w_grouped", tag="slot4", align_bytes=64)
+        for h in range(2):
+            dst = w_grouped[:, :, h * 64 : (h + 1) * 64, :].rearrange("p t m j -> p m j t")
+            src = w_raw[h][:].rearrange("p j (m t) -> p m j t", t=PACK)
+            nc.scalar.activation(dst, src, ACT.Copy)
+
+        cand_bytes = work.tile([P, C], U8, name="cand_bytes", tag="slot3", align_bytes=64)
+        nc.vector.tensor_copy(cand_bytes[:], scale_table[:].indirect(cand_list[:]))
+        dealt_bytes = keep.tile([P, C], U8, name="dealt_bytes", align_bytes=64)
+        nc.vector.tensor_copy(
+            dealt_bytes[:].rearrange("p (t m) -> p m t", t=PACK), cand_bytes[:].rearrange("p (m t) -> p m t", t=PACK)
+        )
+
+        w_codes = keep.tile([P, H], U32, name="w_codes", align_bytes=64)
+        w_scales = keep.tile([P, H], U8, name="w_scales", align_bytes=64)
+        for t in ORDER:
+            cols = slice(t * P, (t + 1) * P)
+            nc.vector.quantize_mx(
+                out=w_codes[:, cols].bitcast(FP8X4),
+                scales=w_scales[:, cols],
+                in_=w_grouped[:, t, :, :].rearrange("p m j -> p (m j)"),
+            )
+        offs_words = keep.tile([P, S], U32, name="offs_words", align_bytes=64)
+        nc.vector.tensor_copy(offs_words[:], word_table[:].indirect(offs_list[:]))
+
+        mem_rows = mem.rearrange("(p t) u -> p t u", t=PACK)
+        page = {}
+        for i, t in enumerate(ORDER):
+            page[t] = work.tile([P, U], F32, name="page%d" % t, tag="slot%d" % i, align_bytes=64)
+            nc.sync.dma_start(page[t][:], mem_rows[:, t, :])
+        cand_scales = place_scale_rows("cand_scales", dealt_bytes, nc.sync)
+
+        th, keep_old, gated_new = {}, {}, {}
+        for t in ORDER:
+            cols = slice(t * P, (t + 1) * P)
+            y = psum.tile([P, S], F32, name="y%d" % t)
+            nc.tensor.matmul_mx(
+                out=y[:],
+                lhsT=w_codes[:, cols].bitcast(FP8X4),
+                lhsT_scale=w_scales[:, cols],
+                rhs=offs_words[:].bitcast(FP8X4),
+                rhs_scale=offs_scales[:],
+                start=True,
+                stop=True,
+            )
+            th[t] = work.tile([P, S], F32, name="th%d" % t)
+            nc.scalar.activation(th[t][:], y[:], ACT.Tanh, scale=-0.5)
+            if t not in (first, last):
+                keep_old[t] = work.tile([P, S], F32, name="keep_old%d" % t)
+                nc.scalar.activation(keep_old[t][:], th[t][:], ACT.Copy, scale=0.5, bias=0.5)
+            gated_new[t] = work.tile([P, S], F32, name="gated_new%d" % t)
+            nc.scalar.activation(gated_new[t][:], y[:], ACT.Silu)
+        nc.scalar.activation(warm[:, 1:2], gated_new[last][:, 0:1], ACT.Sigmoid)
+
+        cand_words = work.tile([P, C], U32, name="cand_words", tag="slot4", align_bytes=64)
+        nc.vector.tensor_copy(cand_words[:], word_table[:].indirect(cand_list[:]))
+        dealt_words = keep.tile([P, C], U32, name="dealt_words", align_bytes=64)
+        nc.vector.tensor_copy(
+            dealt_words[:].rearrange("p (t m) -> p m t", t=PACK), cand_words[:].rearrange("p (m t) -> p m t", t=PACK)
+        )
+
+        z_grouped = [keep.tile([P, HALF, PACK], BF16, name="z_grouped%d" % h, align_bytes=64) for h in range(2)]
+        for t in ORDER:
+            kept = work.tile([P, S], F32, name="kept", bufs=4)
+            if t == first:
+                old_half = work.tile([P, S], F32, name="old_half")
+                nc.vector.tensor_scalar(old_half[:], page[t][:].indirect(n1_list[:]), 0.5, 0.0, ALU.mult, ALU.add)
+                nc.vector.scalar_tensor_tensor(kept[:], th[t][:], 1.0, old_half[:], ALU.add, ALU.mult)
+            else:
+                nc.vector.tensor_tensor(kept[:], page[t][:].indirect(n1_list[:]), keep_old[t][:], ALU.mult)
+            nc.vector.tensor_tensor(page[t][:].indirect(n1_list[:]), kept[:], gated_new[t][:], ALU.add)
+            for h in range(2):
+                src = page[t][:, h * HALF : (h + 1) * HALF]
+                if t == last and h == 0:
+                    nc.vector.tensor_scalar(z_grouped[h][:, :, t], src, gains[:, t : t + 1], None, ALU.mult)
+                else:
+                    nc.scalar.activation(z_grouped[h][:, :, t], src, ACT.Copy, scale=gains[:, t : t + 1])
+            if t == first:
+                keep_old[last] = work.tile([P, S], F32, name="keep_last", tag="gated_new%d" % t)
+                nc.scalar.activation(keep_old[last][:], th[last][:], ACT.Copy, scale=0.5, bias=0.5)
+
+        z_codes, z_scales = [], []
+        for h in range(2):
+            z_codes.append(keep.tile([P, HALF], U32, name="z_codes%d" % h, align_bytes=64))
+            z_scales.append(keep.tile([P, HALF], U8, name="z_scales%d" % h, align_bytes=64))
+            nc.vector.quantize_mx(
+                out=z_codes[h][:].bitcast(FP8X4),
+                scales=z_scales[h][:],
+                in_=z_grouped[h][:].rearrange("p u t -> p (u t)"),
+            )
+
+        out_rows = out.rearrange("(p t) u -> p t u", t=PACK)
+        scores = {}
+
+        def score_tile(t):
+            scores[t] = keep.tile([P, U], F32, name="scores%d" % t)
+            cols = slice(t * P, (t + 1) * P)
+            for h in range(2):
+                sums = psum.tile([P, HALF], F32, name="sums%d%d" % (t % 2, h))
+                nc.tensor.matmul_mx(
+                    out=sums[:],
+                    lhsT=dealt_words[:, cols].bitcast(FP8X4),
+                    lhsT_scale=cand_scales[:, cols],
+                    rhs=z_codes[h][:].bitcast(FP8X4),
+                    rhs_scale=z_scales[h][:],
+                    start=True,
+                    stop=True,
+                )
+                dst = scores[t][:, h * HALF : (h + 1) * HALF]
+                if t == 0 and h == 1:
+                    nc.vector.tensor_scalar(dst, sums[:], 0.0625, None, ALU.mult)
+                else:
+                    nc.scalar.activation(dst, sums[:], ACT.Copy, scale=0.0625)
+
+        steps = [(t, h) for t in range(PACK) for h in range(2)]
+        gate, other, gated = {}, {}, {}
+
+        def fetch(i):
+            t, h = steps[i]
+            if h == 0:
+                score_tile(t)
+            entries = slice(h * HALF // 16, (h + 1) * HALF // 16)
+            gate[i] = work.tile([P, HALF], F32, name="gate", bufs=3)
+            nc.scalar.activation(gate[i][:], scores[t][:].indirect(n2_list[:, entries]), ACT.Sigmoid)
+            other[i] = work.tile([P, HALF], F32, name="other", bufs=3)
+            nc.vector.tensor_copy(other[i][:], scores[t][:].indirect(n3_list[:, entries]))
+
+        def multiply(i):
+            t, h = steps[i]
+            gated[i] = work.tile([P, HALF], F32, name="gated", bufs=3)
+            nc.vector.tensor_tensor(gated[i][:], gate[i][:], scores[t][:, h * HALF : (h + 1) * HALF], ALU.mult)
+
+        def finish(i):
+            t, h = steps[i]
+            result = work.tile([P, HALF], F32, name="result", bufs=4)
+            nc.vector.tensor_tensor(result[:], gated[i][:], other[i][:], ALU.max)
+            nc.sync.dma_start(out_rows[:, t, h * HALF : (h + 1) * HALF], result[:])
+
+        for i in range(len(steps) + 2):
+            if i < len(steps):
+                fetch(i)
+            if i >= 2:
+                finish(i - 2)
+            if 1 <= i <= len(steps):
+                multiply(i - 1)

@@ -16,6 +16,7 @@ P = 128
 PACK = 4
 K, T, S, H, U, C = 512, 2048, 512, 512, 1024, 512
 HALF = U // 2
+QUARTER = U // 4
 FLOPS = 2 * K * H * S + 2 * K * C * U
 ORDER = (2, 0, 1, 3)
 
@@ -35,25 +36,24 @@ def tile_picked_hcandpagetgmax_none_p_kernel(tc, x_words, x_scales, w1, mem, gs,
 
         scale_table = keep.tile([P, T], U8, name="scale_table", align_bytes=64)
         nc.vector.memset(scale_table[:].bitcast(I32), 0)
-        scale_rows = x_scales[0].rearrange("(r e) c -> r e c", e=2)
-        for e in range(2):
-            nc.scalar.dma_start(scale_table[e:P:16, :].bitcast(I32), scale_rows[:, e, :].bitcast(I32))
+        nc.scalar.dma_start(scale_table[0:P:8, :].bitcast(I32), x_scales[0].bitcast(I32))
 
         offs_list = load_list("offs_list", offs)
-        w_rows = w1.rearrange("(p j) c -> p j c", j=PACK)
-        w_raw = []
-        for h in range(2):
-            tile = work.tile([P, PACK, H // 2], F32, name="w_raw%d" % h, tag="slot%d" % h, align_bytes=64)
-            nc.sync.dma_start(tile[:], w_rows[:, :, h * (H // 2) : (h + 1) * (H // 2)])
-            w_raw.append(tile)
         cand_list = load_list("cand_list", cand)
         n1_list = load_list("n1_list", n1)
         gains = keep.tile([P, PACK], F32, name="gains")
         nc.sync.dma_start(gains[:], gs.rearrange("(p t) o -> p (t o)", t=PACK))
-        word_table = keep.tile([P, T], U32, name="word_table", align_bytes=64)
-        nc.sync.dma_start(word_table[:].bitcast(I32), x_words[0].rearrange("p n t -> p (n t)").bitcast(I32))
         n2_list = load_list("n2_list", n2)
         n3_list = load_list("n3_list", n3)
+        w_rows = w1.rearrange("(p j) c -> p j c", j=PACK)
+        w_raw = []
+        for q in range(PACK):
+            tile = work.tile([P, PACK, P], F32, name="w_raw%d" % q, tag="slot%d" % (q - 1), align_bytes=64)
+            nc.sync.dma_start(tile[:], w_rows[:, :, q * P : (q + 1) * P])
+            w_raw.append(tile)
+            if q == 0:
+                word_table = keep.tile([P, T], U32, name="word_table", align_bytes=64)
+                nc.sync.dma_start(word_table[:].bitcast(I32), x_words[0].rearrange("p n t -> p (n t)").bitcast(I32))
 
         warm_in = keep.tile([P, 1], F32, name="warm_in")
         nc.vector.memset(warm_in[:], 0.0)
@@ -62,22 +62,25 @@ def tile_picked_hcandpagetgmax_none_p_kernel(tc, x_words, x_scales, w1, mem, gs,
 
         def place_scale_rows(name, picked, queue):
             plane = keep.tile([P, S], U8, name=name, align_bytes=64)
-            nc.vector.tensor_copy(plane[:].bitcast(I32), picked[:].bitcast(I32))
-            for e in range(2):
-                queue.dma_start(plane[2 + e : P : 32, :].bitcast(I32), picked[16 + e : P : 32, :].bitcast(I32))
+            nc.gpsimd.memset(plane[:], 0)
+            for j in range(4):
+                queue.dma_start(plane[j:P:32, :].bitcast(I32), picked[8 * j : P : 32, :].bitcast(I32))
             return plane
 
-        offs_bytes = work.tile([P, S], U8, name="offs_bytes", tag="slot2", align_bytes=64)
+        offs_bytes = work.tile([P, S], U8, name="offs_bytes", tag="slot3", align_bytes=64)
         nc.vector.tensor_copy(offs_bytes[:], scale_table[:].indirect(offs_list[:]))
         offs_scales = place_scale_rows("offs_scales", offs_bytes, nc.scalar)
 
-        w_grouped = work.tile([P, PACK, P, PACK], BF16, name="w_grouped", tag="slot4", align_bytes=64)
-        for h in range(2):
-            dst = w_grouped[:, :, h * 64 : (h + 1) * 64, :].rearrange("p t m j -> p m j t")
-            src = w_raw[h][:].rearrange("p j (m t) -> p m j t", t=PACK)
+        offs_words = keep.tile([P, S], U32, name="offs_words", align_bytes=64)
+        nc.vector.tensor_copy(offs_words[:], word_table[:].indirect(offs_list[:]))
+
+        w_grouped = keep.tile([P, PACK, P, PACK], BF16, name="w_grouped", align_bytes=64)
+        for q in range(PACK):
+            dst = w_grouped[:, :, q * 32 : (q + 1) * 32, :].rearrange("p t m j -> p m j t")
+            src = w_raw[q][:].rearrange("p j (m t) -> p m j t", t=PACK)
             nc.scalar.activation(dst, src, ACT.Copy)
 
-        cand_bytes = work.tile([P, C], U8, name="cand_bytes", tag="slot3", align_bytes=64)
+        cand_bytes = keep.tile([P, C], U8, name="cand_bytes", align_bytes=64)
         nc.vector.tensor_copy(cand_bytes[:], scale_table[:].indirect(cand_list[:]))
         dealt_bytes = keep.tile([P, C], U8, name="dealt_bytes", align_bytes=64)
         nc.vector.tensor_copy(
@@ -93,8 +96,6 @@ def tile_picked_hcandpagetgmax_none_p_kernel(tc, x_words, x_scales, w1, mem, gs,
                 scales=w_scales[:, cols],
                 in_=w_grouped[:, t, :, :].rearrange("p m j -> p (m j)"),
             )
-        offs_words = keep.tile([P, S], U32, name="offs_words", align_bytes=64)
-        nc.vector.tensor_copy(offs_words[:], word_table[:].indirect(offs_list[:]))
 
         mem_rows = mem.rearrange("(p t) u -> p t u", t=PACK)
         page = {}
@@ -106,7 +107,7 @@ def tile_picked_hcandpagetgmax_none_p_kernel(tc, x_words, x_scales, w1, mem, gs,
         th, keep_old, gated_new = {}, {}, {}
         for t in ORDER:
             cols = slice(t * P, (t + 1) * P)
-            y = psum.tile([P, S], F32, name="y%d" % t)
+            y = psum.tile([P, S], F32, name="y", tag="bank%d" % t)
             nc.tensor.matmul_mx(
                 out=y[:],
                 lhsT=w_codes[:, cols].bitcast(FP8X4),
@@ -125,14 +126,14 @@ def tile_picked_hcandpagetgmax_none_p_kernel(tc, x_words, x_scales, w1, mem, gs,
             nc.scalar.activation(gated_new[t][:], y[:], ACT.Silu)
         nc.scalar.activation(warm[:, 1:2], gated_new[last][:, 0:1], ACT.Sigmoid)
 
-        cand_words = work.tile([P, C], U32, name="cand_words", tag="slot4", align_bytes=64)
+        cand_words = keep.tile([P, C], U32, name="cand_words", align_bytes=64)
         nc.vector.tensor_copy(cand_words[:], word_table[:].indirect(cand_list[:]))
         dealt_words = keep.tile([P, C], U32, name="dealt_words", align_bytes=64)
         nc.vector.tensor_copy(
             dealt_words[:].rearrange("p (t m) -> p m t", t=PACK), cand_words[:].rearrange("p (m t) -> p m t", t=PACK)
         )
 
-        z_grouped = [keep.tile([P, HALF, PACK], BF16, name="z_grouped%d" % h, align_bytes=64) for h in range(2)]
+        z_grouped = keep.tile([P, U, PACK], BF16, name="z_grouped", align_bytes=64)
         for t in ORDER:
             kept = work.tile([P, S], F32, name="kept", bufs=4)
             if t == first:
@@ -142,24 +143,25 @@ def tile_picked_hcandpagetgmax_none_p_kernel(tc, x_words, x_scales, w1, mem, gs,
             else:
                 nc.vector.tensor_tensor(kept[:], page[t][:].indirect(n1_list[:]), keep_old[t][:], ALU.mult)
             nc.vector.tensor_tensor(page[t][:].indirect(n1_list[:]), kept[:], gated_new[t][:], ALU.add)
-            for h in range(2):
-                src = page[t][:, h * HALF : (h + 1) * HALF]
-                if t == last and h == 0:
-                    nc.vector.tensor_scalar(z_grouped[h][:, :, t], src, gains[:, t : t + 1], None, ALU.mult)
+            width = QUARTER if t == last else U
+            for u0 in range(0, U, width):
+                cols = slice(u0, u0 + width)
+                if t == last and u0 % HALF == 0:
+                    nc.vector.tensor_scalar(z_grouped[:, cols, t], page[t][:, cols], gains[:, t : t + 1], None, ALU.mult)
                 else:
-                    nc.scalar.activation(z_grouped[h][:, :, t], src, ACT.Copy, scale=gains[:, t : t + 1])
+                    nc.scalar.activation(z_grouped[:, cols, t], page[t][:, cols], ACT.Copy, scale=gains[:, t : t + 1])
             if t == first:
                 keep_old[last] = work.tile([P, S], F32, name="keep_last", tag="gated_new%d" % t)
                 nc.scalar.activation(keep_old[last][:], th[last][:], ACT.Copy, scale=0.5, bias=0.5)
 
-        z_codes, z_scales = [], []
-        for h in range(2):
-            z_codes.append(keep.tile([P, HALF], U32, name="z_codes%d" % h, align_bytes=64))
-            z_scales.append(keep.tile([P, HALF], U8, name="z_scales%d" % h, align_bytes=64))
+        z_codes = keep.tile([P, U], U32, name="z_codes", align_bytes=64)
+        z_scales = keep.tile([P, U], U8, name="z_scales", align_bytes=64)
+        for q in range(4):
+            cols = slice(q * QUARTER, (q + 1) * QUARTER)
             nc.vector.quantize_mx(
-                out=z_codes[h][:].bitcast(FP8X4),
-                scales=z_scales[h][:],
-                in_=z_grouped[h][:].rearrange("p u t -> p (u t)"),
+                out=z_codes[:, cols].bitcast(FP8X4),
+                scales=z_scales[:, cols],
+                in_=z_grouped[:, cols, :].rearrange("p u t -> p (u t)"),
             )
 
         out_rows = out.rearrange("(p t) u -> p t u", t=PACK)
@@ -167,23 +169,25 @@ def tile_picked_hcandpagetgmax_none_p_kernel(tc, x_words, x_scales, w1, mem, gs,
 
         def score_tile(t):
             scores[t] = keep.tile([P, U], F32, name="scores%d" % t)
-            cols = slice(t * P, (t + 1) * P)
-            for h in range(2):
-                sums = psum.tile([P, HALF], F32, name="sums%d%d" % (t % 2, h))
+            rows = slice(t * P, (t + 1) * P)
+            width = QUARTER if t == 0 else HALF
+            for u0 in range(0, U, width):
+                cols = slice(u0, u0 + width)
+                bank = (u0 + width) // QUARTER - 1
+                sums = psum.tile([P, width], F32, name="sums", tag="bank%d" % bank)
                 nc.tensor.matmul_mx(
                     out=sums[:],
-                    lhsT=dealt_words[:, cols].bitcast(FP8X4),
-                    lhsT_scale=cand_scales[:, cols],
-                    rhs=z_codes[h][:].bitcast(FP8X4),
-                    rhs_scale=z_scales[h][:],
+                    lhsT=dealt_words[:, rows].bitcast(FP8X4),
+                    lhsT_scale=cand_scales[:, rows],
+                    rhs=z_codes[:, cols].bitcast(FP8X4),
+                    rhs_scale=z_scales[:, cols],
                     start=True,
                     stop=True,
                 )
-                dst = scores[t][:, h * HALF : (h + 1) * HALF]
-                if t == 0 and h == 1:
-                    nc.vector.tensor_scalar(dst, sums[:], 0.0625, None, ALU.mult)
+                if t == 0 and bank == 3:
+                    nc.vector.tensor_scalar(scores[t][:, cols], sums[:], 0.0625, None, ALU.mult)
                 else:
-                    nc.scalar.activation(dst, sums[:], ACT.Copy, scale=0.0625)
+                    nc.scalar.activation(scores[t][:, cols], sums[:], ACT.Copy, scale=0.0625)
 
         steps = [(t, h) for t in range(PACK) for h in range(2)]
         gate, other, gated = {}, {}, {}
@@ -201,7 +205,8 @@ def tile_picked_hcandpagetgmax_none_p_kernel(tc, x_words, x_scales, w1, mem, gs,
         def multiply(i):
             t, h = steps[i]
             gated[i] = work.tile([P, HALF], F32, name="gated", bufs=3)
-            nc.vector.tensor_tensor(gated[i][:], gate[i][:], scores[t][:, h * HALF : (h + 1) * HALF], ALU.mult)
+            engine = nc.vector if i == len(steps) - 1 else nc.gpsimd
+            engine.tensor_tensor(gated[i][:], gate[i][:], scores[t][:, h * HALF : (h + 1) * HALF], ALU.mult)
 
         def finish(i):
             t, h = steps[i]

@@ -205,8 +205,7 @@ def tile_picked_hcandpagetgmax_none_p_kernel(tc, x_words, x_scales, w1, mem, gs,
         def multiply(i):
             t, h = steps[i]
             gated[i] = work.tile([P, HALF], F32, name="gated", bufs=3)
-            engine = nc.vector if i == len(steps) - 1 else nc.gpsimd
-            engine.tensor_tensor(gated[i][:], gate[i][:], scores[t][:, h * HALF : (h + 1) * HALF], ALU.mult)
+            nc.vector.tensor_tensor(gated[i][:], gate[i][:], scores[t][:, h * HALF : (h + 1) * HALF], ALU.mult)
 
         def finish(i):
             t, h = steps[i]

@@ -19,6 +19,7 @@ HALF = U // 2
 QUARTER = U // 4
 FLOPS = 2 * K * H * S + 2 * K * C * U
 ORDER = (2, 0, 1, 3)
+SCORE_BANKS = {1: (1, 0), 2: (1, 4), 3: (1, 5)}
 
 
 def tile_picked_hcandpagetgmax_none_p_kernel(tc, x_words, x_scales, w1, mem, gs, offs, n1, cand, n2, n3, out):
@@ -48,7 +49,7 @@ def tile_picked_hcandpagetgmax_none_p_kernel(tc, x_words, x_scales, w1, mem, gs,
         w_rows = w1.rearrange("(p j) c -> p j c", j=PACK)
         w_raw = []
         for q in range(PACK):
-            tile = work.tile([P, PACK, P], F32, name="w_raw%d" % q, tag="slot%d" % (q - 1), align_bytes=64)
+            tile = work.tile([P, PACK, P], F32, name="w_raw%d" % q, tag="slot%d" % q if q else "w_first", align_bytes=64)
             nc.sync.dma_start(tile[:], w_rows[:, :, q * P : (q + 1) * P])
             w_raw.append(tile)
             if q == 0:
@@ -67,20 +68,20 @@ def tile_picked_hcandpagetgmax_none_p_kernel(tc, x_words, x_scales, w1, mem, gs,
                 queue.dma_start(plane[j:P:32, :].bitcast(I32), picked[8 * j : P : 32, :].bitcast(I32))
             return plane
 
-        offs_bytes = work.tile([P, S], U8, name="offs_bytes", tag="slot3", align_bytes=64)
+        offs_bytes = keep.tile([P, S], U8, name="offs_bytes", align_bytes=64)
         nc.vector.tensor_copy(offs_bytes[:], scale_table[:].indirect(offs_list[:]))
         offs_scales = place_scale_rows("offs_scales", offs_bytes, nc.scalar)
 
         offs_words = keep.tile([P, S], U32, name="offs_words", align_bytes=64)
         nc.vector.tensor_copy(offs_words[:], word_table[:].indirect(offs_list[:]))
 
-        w_grouped = keep.tile([P, PACK, P, PACK], BF16, name="w_grouped", align_bytes=64)
+        w_grouped = work.tile([P, PACK, P, PACK], BF16, name="w_grouped", tag="w_grouped", align_bytes=64)
         for q in range(PACK):
             dst = w_grouped[:, :, q * 32 : (q + 1) * 32, :].rearrange("p t m j -> p m j t")
             src = w_raw[q][:].rearrange("p j (m t) -> p m j t", t=PACK)
             nc.scalar.activation(dst, src, ACT.Copy)
 
-        cand_bytes = keep.tile([P, C], U8, name="cand_bytes", align_bytes=64)
+        cand_bytes = work.tile([P, C], U8, name="cand_bytes", tag="slot0", align_bytes=64)
         nc.vector.tensor_copy(cand_bytes[:], scale_table[:].indirect(cand_list[:]))
         dealt_bytes = keep.tile([P, C], U8, name="dealt_bytes", align_bytes=64)
         nc.vector.tensor_copy(
@@ -104,8 +105,13 @@ def tile_picked_hcandpagetgmax_none_p_kernel(tc, x_words, x_scales, w1, mem, gs,
             nc.sync.dma_start(page[t][:], mem_rows[:, t, :])
         cand_scales = place_scale_rows("cand_scales", dealt_bytes, nc.sync)
 
-        th, keep_old, gated_new = {}, {}, {}
-        for t in ORDER:
+        th, keep_old, gated_new, projected = {}, {}, {}, {}
+
+        def silu_tile(t):
+            gated_new[t] = work.tile([P, S], F32, name="gated_new%d" % t)
+            nc.scalar.activation(gated_new[t][:], projected[t][:], ACT.Silu)
+
+        for i, t in enumerate(ORDER):
             cols = slice(t * P, (t + 1) * P)
             y = psum.tile([P, S], F32, name="y", tag="bank%d" % t)
             nc.tensor.matmul_mx(
@@ -119,23 +125,25 @@ def tile_picked_hcandpagetgmax_none_p_kernel(tc, x_words, x_scales, w1, mem, gs,
             )
             th[t] = work.tile([P, S], F32, name="th%d" % t)
             nc.scalar.activation(th[t][:], y[:], ACT.Tanh, scale=-0.5)
-            if t not in (first, last):
+            if t != first:
                 keep_old[t] = work.tile([P, S], F32, name="keep_old%d" % t)
                 nc.scalar.activation(keep_old[t][:], th[t][:], ACT.Copy, scale=0.5, bias=0.5)
-            gated_new[t] = work.tile([P, S], F32, name="gated_new%d" % t)
-            nc.scalar.activation(gated_new[t][:], y[:], ACT.Silu)
+            projected[t] = y
+            if i != 1:
+                silu_tile(ORDER[max(i - 1, 0)])
+        silu_tile(last)
         nc.scalar.activation(warm[:, 1:2], gated_new[last][:, 0:1], ACT.Sigmoid)
 
         cand_words = keep.tile([P, C], U32, name="cand_words", align_bytes=64)
         nc.vector.tensor_copy(cand_words[:], word_table[:].indirect(cand_list[:]))
-        dealt_words = keep.tile([P, C], U32, name="dealt_words", align_bytes=64)
+        dealt_words = work.tile([P, C], U32, name="dealt_words", tag="w_grouped", align_bytes=64)
         nc.vector.tensor_copy(
             dealt_words[:].rearrange("p (t m) -> p m t", t=PACK), cand_words[:].rearrange("p (m t) -> p m t", t=PACK)
         )
 
         z_grouped = keep.tile([P, U, PACK], BF16, name="z_grouped", align_bytes=64)
         for t in ORDER:
-            kept = work.tile([P, S], F32, name="kept", bufs=4)
+            kept = work.tile([P, S], F32, name="kept", tag="slot0" if t == last else "kept%d" % t, align_bytes=64)
             if t == first:
                 old_half = work.tile([P, S], F32, name="old_half")
                 nc.vector.tensor_scalar(old_half[:], page[t][:].indirect(n1_list[:]), 0.5, 0.0, ALU.mult, ALU.add)
@@ -150,9 +158,6 @@ def tile_picked_hcandpagetgmax_none_p_kernel(tc, x_words, x_scales, w1, mem, gs,
                     nc.vector.tensor_scalar(z_grouped[:, cols, t], page[t][:, cols], gains[:, t : t + 1], None, ALU.mult)
                 else:
                     nc.scalar.activation(z_grouped[:, cols, t], page[t][:, cols], ACT.Copy, scale=gains[:, t : t + 1])
-            if t == first:
-                keep_old[last] = work.tile([P, S], F32, name="keep_last", tag="gated_new%d" % t)
-                nc.scalar.activation(keep_old[last][:], th[last][:], ACT.Copy, scale=0.5, bias=0.5)
 
         z_codes = keep.tile([P, U], U32, name="z_codes", align_bytes=64)
         z_scales = keep.tile([P, U], U8, name="z_scales", align_bytes=64)
@@ -165,7 +170,7 @@ def tile_picked_hcandpagetgmax_none_p_kernel(tc, x_words, x_scales, w1, mem, gs,
             )
 
         out_rows = out.rearrange("(p t) u -> p t u", t=PACK)
-        scores = {}
+        scores, sums_of = {}, {}
 
         def score_tile(t):
             scores[t] = keep.tile([P, U], F32, name="scores%d" % t)
@@ -173,8 +178,9 @@ def tile_picked_hcandpagetgmax_none_p_kernel(tc, x_words, x_scales, w1, mem, gs,
             width = QUARTER if t == 0 else HALF
             for u0 in range(0, U, width):
                 cols = slice(u0, u0 + width)
-                bank = (u0 + width) // QUARTER - 1
+                bank = u0 // QUARTER if t == 0 else SCORE_BANKS[t][u0 // HALF]
                 sums = psum.tile([P, width], F32, name="sums", tag="bank%d" % bank)
+                sums_of[t, u0] = sums
                 nc.tensor.matmul_mx(
                     out=sums[:],
                     lhsT=dealt_words[:, rows].bitcast(FP8X4),
@@ -189,34 +195,44 @@ def tile_picked_hcandpagetgmax_none_p_kernel(tc, x_words, x_scales, w1, mem, gs,
                 else:
                     nc.scalar.activation(scores[t][:, cols], sums[:], ACT.Copy, scale=0.0625)
 
-        steps = [(t, h) for t in range(PACK) for h in range(2)]
         gate, other, gated = {}, {}, {}
 
-        def fetch(i):
-            t, h = steps[i]
-            if h == 0:
-                score_tile(t)
-            entries = slice(h * HALF // 16, (h + 1) * HALF // 16)
-            gate[i] = work.tile([P, HALF], F32, name="gate", bufs=3)
-            nc.scalar.activation(gate[i][:], scores[t][:].indirect(n2_list[:, entries]), ACT.Sigmoid)
-            other[i] = work.tile([P, HALF], F32, name="other", bufs=3)
-            nc.vector.tensor_copy(other[i][:], scores[t][:].indirect(n3_list[:, entries]))
+        def fetch(t):
+            gate[t] = work.tile([P, U], F32, name="gate", bufs=2)
+            other[t] = work.tile([P, U], F32, name="other", bufs=2)
+            for h in range(2):
+                cols = slice(h * HALF, (h + 1) * HALF)
+                entries = slice(h * HALF // 16, (h + 1) * HALF // 16)
+                nc.scalar.activation(gate[t][:, cols], scores[t][:].indirect(n2_list[:, entries]), ACT.Sigmoid)
+                nc.vector.tensor_copy(other[t][:, cols], scores[t][:].indirect(n3_list[:, entries]))
+                if h == 0 and t + 1 < PACK:
+                    score_tile(t + 1)
 
-        def multiply(i):
-            t, h = steps[i]
-            gated[i] = work.tile([P, HALF], F32, name="gated", bufs=3)
-            nc.vector.tensor_tensor(gated[i][:], gate[i][:], scores[t][:, h * HALF : (h + 1) * HALF], ALU.mult)
+        def multiply(t):
+            if t < PACK - 1:
+                products = work.tile([P, U if t < PACK - 2 else 2 * U], F32, name="products")
+                gated[t] = products[:, 0:U]
+                if t == PACK - 2:
+                    gated[t + 1] = products[:, U : 2 * U]
+            nc.gpsimd.tensor_tensor(gated[t][:, 0:HALF], gate[t][:, 0:HALF], scores[t][:, 0:HALF], ALU.mult)
+            width = QUARTER if t == 0 else HALF
+            for u0 in range(HALF, U, width):
+                cols = slice(u0, u0 + width)
+                nc.vector.scalar_tensor_tensor(
+                    gated[t][:, cols], sums_of[t, u0][:], 0.0625, gate[t][:, cols], ALU.mult, ALU.mult
+                )
 
-        def finish(i):
-            t, h = steps[i]
-            result = work.tile([P, HALF], F32, name="result", bufs=4)
-            nc.vector.tensor_tensor(result[:], gated[i][:], other[i][:], ALU.max)
-            nc.sync.dma_start(out_rows[:, t, h * HALF : (h + 1) * HALF], result[:])
+        def finish(t):
+            edges = (0, HALF, U) if t < PACK - 1 else (0, HALF, HALF + QUARTER, U)
+            for u0, u1 in zip(edges, edges[1:]):
+                result = work.tile([P, u1 - u0], F32, name="result%d_%d" % (t, u0))
+                nc.vector.tensor_tensor(result[:], gated[t][:, u0:u1], other[t][:, u0:u1], ALU.max)
+                nc.sync.dma_start(out_rows[:, t, u0:u1], result[:])
 
-        for i in range(len(steps) + 2):
-            if i < len(steps):
-                fetch(i)
-            if i >= 2:
-                finish(i - 2)
-            if 1 <= i <= len(steps):
-                multiply(i - 1)
+        score_tile(0)
+        for t in range(PACK + 1):
+            if t < PACK:
+                fetch(t)
+            if t >= 1:
+                multiply(t - 1)
+                finish(t - 1)

from contextlib import ExitStack

import concourse.mybir as mybir

F32 = mybir.dt.float32
BF16 = mybir.dt.bfloat16
I32 = mybir.dt.int32
U32 = mybir.dt.uint32
U16 = mybir.dt.uint16
U8 = mybir.dt.uint8
FP8X4 = mybir.dt.float8_e4m3fn_x4
ACT = mybir.ActivationFunctionType
ALU = mybir.AluOpType

P = 128
PACK = 4
K, T, S, H, U, C = 512, 2048, 512, 512, 1024, 512
HALF = U // 2
QUARTER = U // 4
FLOPS = 2 * K * H * S + 2 * K * C * U
ORDER = (2, 0, 1, 3)
SCORE_BANKS = {1: (1, 0), 2: (1, 4), 3: (1, 5)}


def tile_picked_hcandpagetgmax_none_p_kernel(tc, x_words, x_scales, w1, mem, gs, offs, n1, cand, n2, n3, out):
    nc = tc.nc
    first, last = ORDER[0], ORDER[-1]
    with ExitStack() as ctx:
        keep = ctx.enter_context(tc.tile_pool(name="keep", bufs=1))
        work = ctx.enter_context(tc.tile_pool(name="work", bufs=1))
        psum = ctx.enter_context(tc.psum_pool(name="psum", bufs=1))

        def load_list(name, src):
            tile = keep.tile(list(src.shape), U16, name=name)
            nc.sync.dma_start(tile[:], src)
            return tile

        scale_table = keep.tile([P, T], U8, name="scale_table", align_bytes=64)
        nc.vector.memset(scale_table[:].bitcast(I32), 0)
        nc.scalar.dma_start(scale_table[0:P:8, :].bitcast(I32), x_scales[0].bitcast(I32))

        offs_list = load_list("offs_list", offs)
        cand_list = load_list("cand_list", cand)
        n1_list = load_list("n1_list", n1)
        gains = keep.tile([P, PACK], F32, name="gains")
        nc.sync.dma_start(gains[:], gs.rearrange("(p t) o -> p (t o)", t=PACK))
        n2_list = load_list("n2_list", n2)
        n3_list = load_list("n3_list", n3)
        w_rows = w1.rearrange("(p j) c -> p j c", j=PACK)
        w_raw = []
        for q in range(PACK):
            tile = work.tile([P, PACK, P], F32, name="w_raw%d" % q, tag="slot%d" % q if q else "w_first", align_bytes=64)
            nc.sync.dma_start(tile[:], w_rows[:, :, q * P : (q + 1) * P])
            w_raw.append(tile)
            if q == 0:
                word_table = keep.tile([P, T], U32, name="word_table", align_bytes=64)
                nc.sync.dma_start(word_table[:].bitcast(I32), x_words[0].rearrange("p n t -> p (n t)").bitcast(I32))

        warm_in = keep.tile([P, 1], F32, name="warm_in")
        nc.vector.memset(warm_in[:], 0.0)
        warm = keep.tile([P, 2], F32, name="warm")
        nc.scalar.activation(warm[:, 0:1], warm_in[:], ACT.Silu)

        def place_scale_rows(name, picked, queue):
            plane = keep.tile([P, S], U8, name=name, align_bytes=64)
            nc.gpsimd.memset(plane[:], 0)
            for j in range(4):
                queue.dma_start(plane[j:P:32, :].bitcast(I32), picked[8 * j : P : 32, :].bitcast(I32))
            return plane

        offs_bytes = keep.tile([P, S], U8, name="offs_bytes", align_bytes=64)
        nc.vector.tensor_copy(offs_bytes[:], scale_table[:].indirect(offs_list[:]))
        offs_scales = place_scale_rows("offs_scales", offs_bytes, nc.scalar)

        offs_words = keep.tile([P, S], U32, name="offs_words", align_bytes=64)
        nc.vector.tensor_copy(offs_words[:], word_table[:].indirect(offs_list[:]))

        w_grouped = work.tile([P, PACK, P, PACK], BF16, name="w_grouped", tag="w_grouped", align_bytes=64)
        for q in range(PACK):
            dst = w_grouped[:, :, q * 32 : (q + 1) * 32, :].rearrange("p t m j -> p m j t")
            src = w_raw[q][:].rearrange("p j (m t) -> p m j t", t=PACK)
            nc.scalar.activation(dst, src, ACT.Copy)

        cand_bytes = work.tile([P, C], U8, name="cand_bytes", tag="slot0", align_bytes=64)
        nc.vector.tensor_copy(cand_bytes[:], scale_table[:].indirect(cand_list[:]))
        dealt_bytes = keep.tile([P, C], U8, name="dealt_bytes", align_bytes=64)
        nc.vector.tensor_copy(
            dealt_bytes[:].rearrange("p (t m) -> p m t", t=PACK), cand_bytes[:].rearrange("p (m t) -> p m t", t=PACK)
        )

        w_codes = keep.tile([P, H], U32, name="w_codes", align_bytes=64)
        w_scales = keep.tile([P, H], U8, name="w_scales", align_bytes=64)
        for t in ORDER:
            cols = slice(t * P, (t + 1) * P)
            nc.vector.quantize_mx(
                out=w_codes[:, cols].bitcast(FP8X4),
                scales=w_scales[:, cols],
                in_=w_grouped[:, t, :, :].rearrange("p m j -> p (m j)"),
            )

        mem_rows = mem.rearrange("(p t) u -> p t u", t=PACK)
        page = {}
        for i, t in enumerate(ORDER):
            page[t] = work.tile([P, U], F32, name="page%d" % t, tag="slot%d" % i, align_bytes=64)
            nc.sync.dma_start(page[t][:], mem_rows[:, t, :])
        cand_scales = place_scale_rows("cand_scales", dealt_bytes, nc.sync)

        th, keep_old, gated_new, projected = {}, {}, {}, {}

        def silu_tile(t):
            gated_new[t] = work.tile([P, S], F32, name="gated_new%d" % t)
            nc.scalar.activation(gated_new[t][:], projected[t][:], ACT.Silu)

        for i, t in enumerate(ORDER):
            cols = slice(t * P, (t + 1) * P)
            y = psum.tile([P, S], F32, name="y", tag="bank%d" % t)
            nc.tensor.matmul_mx(
                out=y[:],
                lhsT=w_codes[:, cols].bitcast(FP8X4),
                lhsT_scale=w_scales[:, cols],
                rhs=offs_words[:].bitcast(FP8X4),
                rhs_scale=offs_scales[:],
                start=True,
                stop=True,
            )
            th[t] = work.tile([P, S], F32, name="th%d" % t)
            nc.scalar.activation(th[t][:], y[:], ACT.Tanh, scale=-0.5)
            if t != first:
                keep_old[t] = work.tile([P, S], F32, name="keep_old%d" % t)
                nc.scalar.activation(keep_old[t][:], th[t][:], ACT.Copy, scale=0.5, bias=0.5)
            projected[t] = y
            if i != 1:
                silu_tile(ORDER[max(i - 1, 0)])
        silu_tile(last)
        nc.scalar.activation(warm[:, 1:2], gated_new[last][:, 0:1], ACT.Sigmoid)

        cand_words = keep.tile([P, C], U32, name="cand_words", align_bytes=64)
        nc.vector.tensor_copy(cand_words[:], word_table[:].indirect(cand_list[:]))
        dealt_words = work.tile([P, C], U32, name="dealt_words", tag="w_grouped", align_bytes=64)
        nc.vector.tensor_copy(
            dealt_words[:].rearrange("p (t m) -> p m t", t=PACK), cand_words[:].rearrange("p (m t) -> p m t", t=PACK)
        )

        z_grouped = keep.tile([P, U, PACK], BF16, name="z_grouped", align_bytes=64)
        for t in ORDER:
            kept = work.tile([P, S], F32, name="kept", tag="slot0" if t == last else "kept%d" % t, align_bytes=64)
            if t == first:
                old_half = work.tile([P, S], F32, name="old_half")
                nc.vector.tensor_scalar(old_half[:], page[t][:].indirect(n1_list[:]), 0.5, 0.0, ALU.mult, ALU.add)
                nc.vector.scalar_tensor_tensor(kept[:], th[t][:], 1.0, old_half[:], ALU.add, ALU.mult)
            else:
                nc.vector.tensor_tensor(kept[:], page[t][:].indirect(n1_list[:]), keep_old[t][:], ALU.mult)
            nc.vector.tensor_tensor(page[t][:].indirect(n1_list[:]), kept[:], gated_new[t][:], ALU.add)
            width = QUARTER if t == last else U
            for u0 in range(0, U, width):
                cols = slice(u0, u0 + width)
                if t == last and u0 % HALF == 0:
                    nc.vector.tensor_scalar(z_grouped[:, cols, t], page[t][:, cols], gains[:, t : t + 1], None, ALU.mult)
                else:
                    nc.scalar.activation(z_grouped[:, cols, t], page[t][:, cols], ACT.Copy, scale=gains[:, t : t + 1])

        z_codes = keep.tile([P, U], U32, name="z_codes", align_bytes=64)
        z_scales = keep.tile([P, U], U8, name="z_scales", align_bytes=64)
        for q in range(4):
            cols = slice(q * QUARTER, (q + 1) * QUARTER)
            nc.vector.quantize_mx(
                out=z_codes[:, cols].bitcast(FP8X4),
                scales=z_scales[:, cols],
                in_=z_grouped[:, cols, :].rearrange("p u t -> p (u t)"),
            )

        out_rows = out.rearrange("(p t) u -> p t u", t=PACK)
        scores, sums_of = {}, {}

        def score_tile(t):
            scores[t] = keep.tile([P, U], F32, name="scores%d" % t)
            rows = slice(t * P, (t + 1) * P)
            width = QUARTER if t == 0 else HALF
            for u0 in range(0, U, width):
                cols = slice(u0, u0 + width)
                bank = u0 // QUARTER if t == 0 else SCORE_BANKS[t][u0 // HALF]
                sums = psum.tile([P, width], F32, name="sums", tag="bank%d" % bank)
                sums_of[t, u0] = sums
                nc.tensor.matmul_mx(
                    out=sums[:],
                    lhsT=dealt_words[:, rows].bitcast(FP8X4),
                    lhsT_scale=cand_scales[:, rows],
                    rhs=z_codes[:, cols].bitcast(FP8X4),
                    rhs_scale=z_scales[:, cols],
                    start=True,
                    stop=True,
                )
                if t == 0 and bank == 3:
                    nc.vector.tensor_scalar(scores[t][:, cols], sums[:], 0.0625, None, ALU.mult)
                else:
                    nc.scalar.activation(scores[t][:, cols], sums[:], ACT.Copy, scale=0.0625)

        gate, other, gated = {}, {}, {}

        def fetch(t):
            gate[t] = work.tile([P, U], F32, name="gate", bufs=2)
            other[t] = work.tile([P, U], F32, name="other", bufs=2)
            for h in range(2):
                cols = slice(h * HALF, (h + 1) * HALF)
                entries = slice(h * HALF // 16, (h + 1) * HALF // 16)
                nc.scalar.activation(gate[t][:, cols], scores[t][:].indirect(n2_list[:, entries]), ACT.Sigmoid)
                nc.vector.tensor_copy(other[t][:, cols], scores[t][:].indirect(n3_list[:, entries]))
                if h == 0 and t + 1 < PACK:
                    score_tile(t + 1)

        def multiply(t):
            if t < PACK - 1:
                products = work.tile([P, U if t < PACK - 2 else 2 * U], F32, name="products")
                gated[t] = products[:, 0:U]
                if t == PACK - 2:
                    gated[t + 1] = products[:, U : 2 * U]
            nc.gpsimd.tensor_tensor(gated[t][:, 0:HALF], gate[t][:, 0:HALF], scores[t][:, 0:HALF], ALU.mult)
            width = QUARTER if t == 0 else HALF
            for u0 in range(HALF, U, width):
                cols = slice(u0, u0 + width)
                nc.vector.scalar_tensor_tensor(
                    gated[t][:, cols], sums_of[t, u0][:], 0.0625, gate[t][:, cols], ALU.mult, ALU.mult
                )

        def finish(t):
            edges = (0, HALF, U) if t < PACK - 1 else (0, HALF, HALF + QUARTER, U)
            for u0, u1 in zip(edges, edges[1:]):
                result = work.tile([P, u1 - u0], F32, name="result%d_%d" % (t, u0))
                nc.vector.tensor_tensor(result[:], gated[t][:, u0:u1], other[t][:, u0:u1], ALU.max)
                nc.sync.dma_start(out_rows[:, t, u0:u1], result[:])

        score_tile(0)
        for t in range(PACK + 1):
            if t < PACK:
                fetch(t)
            if t >= 1:
                multiply(t - 1)
                finish(t - 1)
